import numpy as np
import ml_dtypes


def mxq(x, axis, fmt="e4m3"):
    dtype, down = {"e4m3": (ml_dtypes.float8_e4m3fn, 7), "e5m2": (ml_dtypes.float8_e5m2, 14)}[fmt]
    v = np.moveaxis(np.asarray(x, np.float32).astype(ml_dtypes.bfloat16).astype(np.float64), axis, -1)
    blocks = v.reshape(v.shape[:-1] + (-1, 32))
    amax = np.abs(blocks).max(-1, keepdims=True)
    byte = np.maximum(np.where(amax > 0, np.frexp(amax)[1] - 1 + 127, 0) - down, 1)
    scale = np.exp2(byte - 127.0)
    codes = (blocks / scale).astype(np.float32).astype(dtype).astype(np.float64)
    return np.moveaxis((codes * scale).reshape(v.shape), -1, axis)


WIDE = False


def mx_kscale(k):
    if not WIDE:
        return np.ones(k)
    levels = np.array([10, -10, 5, -5, 0])
    if k % 512:
        return np.exp2(np.random.permutation(np.resize(levels, k // 32))).repeat(32)
    a = np.empty((k // 512, 16))
    for p in range(k // 512):
        a[p, :8] = np.random.permutation(np.resize(levels, 8))
        for g in range(8):
            far = levels[np.abs(levels - a[p, g]) >= 10]
            a[p, g + 8] = far[np.random.randint(len(far))]
    return np.exp2(a.ravel()).repeat(32)


def f64(x):
    return np.asarray(x).astype(np.float64)


def striped(idx):
    return np.tile(idx.reshape(-1, 16).T, (8, 1)).astype(np.uint16)


def unstriped(offs):
    return offs[:16].T.reshape(-1).astype(np.int64)


def pack_weight(w):
    k, n = w.shape
    w = f64(np.asarray(w, np.float32).astype(ml_dtypes.bfloat16)).reshape(k // 32, 32, n)
    amax = np.abs(w).max(1)
    byte = np.clip(np.where(amax > 0, np.frexp(amax)[1] - 1 + 127 - 7, 1), 1, 254)
    scaled = (w * np.exp2(127.0 - byte)[:, None, :]).reshape(k, n).astype(np.float32)
    words = np.ascontiguousarray(scaled.reshape(k // 512, 128, 4, n).transpose(0, 1, 3, 2)).astype(ml_dtypes.float8_e4m3fn).view(np.uint8)
    return words, np.ascontiguousarray(byte.astype(np.uint8).reshape(k // 512, 16, n))


def unpack_weight(words, scales):
    g, p, n, _ = words.shape
    vals = np.ascontiguousarray(words).view(ml_dtypes.float8_e4m3fn).astype(np.float64) * np.repeat(np.exp2(scales.astype(np.float64) - 127.0), 8, axis=1)[..., None]
    return vals.transpose(0, 1, 3, 2).reshape(g * 512, n)


K, T, E, C, N = 512, 2048, 2, 256, 128


def by_expert(wq, xq):
    return np.concatenate([wq[e].T @ xq[:, e * C:(e + 1) * C] for e in range(E)], axis=1)


def setup_inputs():
    n = np.random.standard_normal
    s = mx_kscale(K)[:, None]
    packed = [pack_weight(m) for m in n((E, K, N)) / np.sqrt(K) / s[None]]
    return {
        "xT": (n((K, T)) * s).astype(np.float32),
        "w_words": np.stack([m[0] for m in packed]),
        "w_scales": np.stack([m[1] for m in packed]),
        "gate": np.tile(np.random.uniform(0.2, 1.0, E * C), (N, 1)).astype(np.float32),
        "offs": striped(np.random.permutation(T)[:E * C]),
    }


def reference(xT, w_words, w_scales, gate, offs):
    idx = unstriped(offs)
    xq = mxq(f64(xT)[:, idx], 0, "e4m3")
    w = np.stack([unpack_weight(w_words[e], w_scales[e]) for e in range(E)])
    y = by_expert(w, xq)
    out = np.zeros((N, T))
    out[:, idx] = f64(gate) * y
    return out

@@ -1,0 +1,104 @@
+from contextlib import ExitStack
+
+import concourse.mybir as mybir
+
+K, T, E, C, N = 512, 2048, 2, 256, 128
+FLOPS = 2 * K * N * E * C
+
+F32 = mybir.dt.float32
+BF16 = mybir.dt.bfloat16
+I32 = mybir.dt.int32
+U32 = mybir.dt.uint32
+U16 = mybir.dt.uint16
+U8 = mybir.dt.uint8
+FP8X4 = mybir.dt.float8_e4m3fn_x4
+
+P = 128
+PACK = 4
+OVERLAP = 2
+LIST_COLS = C // 16
+
+
+def tile_routed_moe_kernel(tc, xT, w_words, w_scales, gate, offs, out):
+    nc = tc.nc
+    mult = mybir.AluOpType.mult
+
+    with ExitStack() as ctx:
+        keep = ctx.enter_context(tc.tile_pool(name="keep", bufs=1))
+        psum = ctx.enter_context(tc.psum_pool(name="psum", bufs=1))
+
+        offsets = keep.tile([P, E * LIST_COLS], U16, name="offsets")
+        nc.sync.dma_start(offsets[:], offs)
+
+        w_scale = keep.tile([P, E * N], U8, name="w_scale", align_bytes=64)
+        nc.vector.memset(w_scale[:].bitcast(I32), 0)
+        scale_rows = w_scales.rearrange("e a (q r) n -> r q (e a) n", r=4)
+
+        planes = xT.rearrange("(p t) n -> t p n", t=PACK)
+        x_plane = []
+        for t in range(PACK):
+            xp = keep.tile([P, T], F32, name="x_plane%d" % t)
+            nc.sync.dma_start(xp[:], planes[t])
+            x_plane.append(xp)
+            if t == 1:
+                for r in range(4):
+                    nc.sync.dma_start(
+                        w_scale[r:P:32, :].rearrange("q (e n) -> q e n", e=E).bitcast(I32),
+                        scale_rows[r].bitcast(I32),
+                    )
+
+        w_code = keep.tile([P, E, PACK * N], U8, name="w_code", align_bytes=64)
+        nc.sync.dma_start(
+            w_code[:].bitcast(I32),
+            w_words.rearrange("e a p n r -> p (e a) (n r)").bitcast(I32),
+        )
+
+        gate_sb = keep.tile([P, E * C], F32, name="gate_sb")
+        nc.sync.dma_start(gate_sb[:], gate)
+
+        window = keep.tile([P, T], F32, name="window")
+        nc.vector.memset(window[:], 0.0)
+
+        warm_in = keep.tile([P, 1], F32, name="warm_in")
+        warm_out = keep.tile([P, 1], F32, name="warm_out")
+        nc.vector.memset(warm_in[:], 0.0)
+        nc.scalar.copy(warm_out[:], warm_in[:])
+
+        grouped = keep.tile([P, E * C, PACK], BF16, name="grouped", align_bytes=64)
+        x_code = [keep.tile([P, C], U32, name="x_code%d" % e, align_bytes=64) for e in range(E)]
+        x_scale = [keep.tile([P, C], U8, name="x_scale%d" % e, align_bytes=64) for e in range(E)]
+        acc = [psum.tile([P, C], F32, name="acc%d" % e) for e in range(E)]
+        y = [keep.tile([P, C], F32, name="y%d" % e) for e in range(E)]
+
+        def slots(e):
+            return offsets[:, e * LIST_COLS:(e + 1) * LIST_COLS]
+
+        def gather(t, col0, col1):
+            nc.vector.tensor_copy(grouped[:, 16 * col0:16 * col1, t], x_plane[t][:].indirect(offsets[:, col0:col1]))
+
+        for t in range(PACK - 1):
+            for e in range(E):
+                gather(t, e * LIST_COLS, (e + 1) * LIST_COLS)
+
+        for e in range(E):
+            gather(PACK - 1, e * LIST_COLS - (OVERLAP if e else 0), (e + 1) * LIST_COLS)
+            nc.vector.quantize_mx(
+                out=x_code[e][:].bitcast(FP8X4),
+                scales=x_scale[e][:],
+                in_=grouped[:, e * C:(e + 1) * C, :].rearrange("p c t -> p (c t)"),
+            )
+            nc.tensor.matmul_mx(
+                out=acc[e][:],
+                lhsT=w_code[:, e, :].bitcast(FP8X4),
+                lhsT_scale=w_scale[:, e * N:(e + 1) * N],
+                rhs=x_code[e][:].bitcast(FP8X4),
+                rhs_scale=x_scale[e][:],
+                start=True,
+                stop=True,
+            )
+            nc.scalar.copy(y[e][:], acc[e][:])
+
+        for e in range(E):
+            nc.vector.tensor_tensor(window[:].indirect(slots(e)), y[e][:], gate_sb[:, e * C:(e + 1) * C], mult)
+
+        nc.sync.dma_start(out, window[:])

@@ -28,7 +28,6 @@ def tile_routed_moe_kernel(tc, xT, w_words, w_scales, gate, offs, out):
         psum = ctx.enter_context(tc.psum_pool(name="psum", bufs=1))
 
         offsets = keep.tile([P, E * LIST_COLS], U16, name="offsets")
-        nc.sync.dma_start(offsets[:], offs)
 
         w_scale = keep.tile([P, E * N], U8, name="w_scale", align_bytes=64)
         nc.vector.memset(w_scale[:].bitcast(I32), 0)
@@ -40,6 +39,8 @@ def tile_routed_moe_kernel(tc, xT, w_words, w_scales, gate, offs, out):
             xp = keep.tile([P, T], F32, name="x_plane%d" % t)
             nc.sync.dma_start(xp[:], planes[t])
             x_plane.append(xp)
+            if t == 0:
+                nc.sync.dma_start(offsets[:], offs)
             if t == 1:
                 for r in range(4):
                     nc.sync.dma_start(

@@ -15,7 +15,7 @@ FP8X4 = mybir.dt.float8_e4m3fn_x4
 
 P = 128
 PACK = 4
-OVERLAP = 2
+PIECE = 128
 LIST_COLS = C // 16
 
 
@@ -66,9 +66,9 @@ def tile_routed_moe_kernel(tc, xT, w_words, w_scales, gate, offs, out):
         nc.scalar.copy(warm_out[:], warm_in[:])
 
         grouped = keep.tile([P, E * C, PACK], BF16, name="grouped", align_bytes=64)
-        x_code = [keep.tile([P, C], U32, name="x_code%d" % e, align_bytes=64) for e in range(E)]
-        x_scale = [keep.tile([P, C], U8, name="x_scale%d" % e, align_bytes=64) for e in range(E)]
-        acc = [psum.tile([P, C], F32, name="acc%d" % e) for e in range(E)]
+        x_code = keep.tile([P, E * C], U32, name="x_code", align_bytes=64)
+        x_scale = keep.tile([P, E * C], U8, name="x_scale", align_bytes=64)
+        acc = [psum.tile([P, PIECE], F32, name="acc%d" % i) for i in range(E * C // PIECE)]
         y = [keep.tile([P, C], F32, name="y%d" % e) for e in range(E)]
 
         def slots(e):
@@ -82,22 +82,26 @@ def tile_routed_moe_kernel(tc, xT, w_words, w_scales, gate, offs, out):
                 gather(t, e * LIST_COLS, (e + 1) * LIST_COLS)
 
         for e in range(E):
-            gather(PACK - 1, e * LIST_COLS - (OVERLAP if e else 0), (e + 1) * LIST_COLS)
+            gather(PACK - 1, e * LIST_COLS, (e + 1) * LIST_COLS)
+
+        for i in range(E * C // PIECE):
+            e = i * PIECE // C
+            cols = slice(i * PIECE, (i + 1) * PIECE)
             nc.vector.quantize_mx(
-                out=x_code[e][:].bitcast(FP8X4),
-                scales=x_scale[e][:],
-                in_=grouped[:, e * C:(e + 1) * C, :].rearrange("p c t -> p (c t)"),
+                out=x_code[:, cols].bitcast(FP8X4),
+                scales=x_scale[:, cols],
+                in_=grouped[:, cols, :].rearrange("p c t -> p (c t)"),
             )
             nc.tensor.matmul_mx(
-                out=acc[e][:],
+                out=acc[i][:],
                 lhsT=w_code[:, e, :].bitcast(FP8X4),
                 lhsT_scale=w_scale[:, e * N:(e + 1) * N],
-                rhs=x_code[e][:].bitcast(FP8X4),
-                rhs_scale=x_scale[e][:],
+                rhs=x_code[:, cols].bitcast(FP8X4),
+                rhs_scale=x_scale[:, cols],
                 start=True,
                 stop=True,
             )
-            nc.scalar.copy(y[e][:], acc[e][:])
+            nc.scalar.copy(y[e][:, i * PIECE - e * C:(i + 1) * PIECE - e * C], acc[i][:])
 
         for e in range(E):
             nc.vector.tensor_tensor(window[:].indirect(slots(e)), y[e][:], gate_sb[:, e * C:(e + 1) * C], mult)

@@ -78,8 +78,7 @@ def tile_routed_moe_kernel(tc, xT, w_words, w_scales, gate, offs, out):
             nc.vector.tensor_copy(grouped[:, 16 * col0:16 * col1, t], x_plane[t][:].indirect(offsets[:, col0:col1]))
 
         for t in range(PACK - 1):
-            for e in range(E):
-                gather(t, e * LIST_COLS, (e + 1) * LIST_COLS)
+            gather(t, 0, E * LIST_COLS)
 
         for e in range(E):
             gather(PACK - 1, e * LIST_COLS, (e + 1) * LIST_COLS)

@@ -15,92 +15,89 @@ FP8X4 = mybir.dt.float8_e4m3fn_x4
 
 P = 128
 PACK = 4
-PIECE = 128
 LIST_COLS = C // 16
+PIECES = [(0, 0, 128), (0, 128, 256), (1, 256, 512)]
+CHUNKS = [0, 1024, 1536, 2048]
 
 
 def tile_routed_moe_kernel(tc, xT, w_words, w_scales, gate, offs, out):
     nc = tc.nc
     mult = mybir.AluOpType.mult
+    copy = mybir.ActivationFunctionType.Copy
 
     with ExitStack() as ctx:
         keep = ctx.enter_context(tc.tile_pool(name="keep", bufs=1))
         psum = ctx.enter_context(tc.psum_pool(name="psum", bufs=1))
 
         offsets = keep.tile([P, E * LIST_COLS], U16, name="offsets")
-
         w_scale = keep.tile([P, E * N], U8, name="w_scale", align_bytes=64)
-        nc.vector.memset(w_scale[:].bitcast(I32), 0)
         scale_rows = w_scales.rearrange("e a (q r) n -> r q (e a) n", r=4)
 
         planes = xT.rearrange("(p t) n -> t p n", t=PACK)
-        x_plane = []
-        for t in range(PACK):
-            xp = keep.tile([P, T], F32, name="x_plane%d" % t)
-            nc.sync.dma_start(xp[:], planes[t])
-            x_plane.append(xp)
-            if t == 0:
-                nc.sync.dma_start(offsets[:], offs)
-            if t == 1:
-                for r in range(4):
-                    nc.sync.dma_start(
-                        w_scale[r:P:32, :].rearrange("q (e n) -> q e n", e=E).bitcast(I32),
-                        scale_rows[r].bitcast(I32),
-                    )
+        x_plane = [keep.tile([P, T], F32, name="x_plane%d" % t) for t in range(PACK)]
+
+        nc.sync.dma_start(x_plane[2][:], planes[2])
+        nc.sync.dma_start(offsets[:], offs)
+        nc.sync.dma_start(x_plane[0][:], planes[0])
+        for r in range(4):
+            nc.sync.dma_start(
+                w_scale[r:P:32, :].rearrange("q (e n) -> q e n", e=E).bitcast(I32),
+                scale_rows[r].bitcast(I32),
+            )
+        nc.sync.dma_start(x_plane[1][:], planes[1])
+        for lo, hi in zip(CHUNKS, CHUNKS[1:]):
+            nc.sync.dma_start(x_plane[3][:, lo:hi], planes[3][:, lo:hi])
 
         w_code = keep.tile([P, E, PACK * N], U8, name="w_code", align_bytes=64)
         nc.sync.dma_start(
             w_code[:].bitcast(I32),
             w_words.rearrange("e a p n r -> p (e a) (n r)").bitcast(I32),
         )
-
         gate_sb = keep.tile([P, E * C], F32, name="gate_sb")
         nc.sync.dma_start(gate_sb[:], gate)
 
         window = keep.tile([P, T], F32, name="window")
         nc.vector.memset(window[:], 0.0)
 
-        warm_in = keep.tile([P, 1], F32, name="warm_in")
-        warm_out = keep.tile([P, 1], F32, name="warm_out")
-        nc.vector.memset(warm_in[:], 0.0)
-        nc.scalar.copy(warm_out[:], warm_in[:])
-
+        x_half2 = keep.tile([P, T], BF16, name="x_half2")
+        x_half3 = keep.tile([P, T], BF16, name="x_half3")
         grouped = keep.tile([P, E * C, PACK], BF16, name="grouped", align_bytes=64)
         x_code = keep.tile([P, E * C], U32, name="x_code", align_bytes=64)
         x_scale = keep.tile([P, E * C], U8, name="x_scale", align_bytes=64)
-        acc = [psum.tile([P, PIECE], F32, name="acc%d" % i) for i in range(E * C // PIECE)]
         y = [keep.tile([P, C], F32, name="y%d" % e) for e in range(E)]
 
         def slots(e):
             return offsets[:, e * LIST_COLS:(e + 1) * LIST_COLS]
 
-        def gather(t, col0, col1):
-            nc.vector.tensor_copy(grouped[:, 16 * col0:16 * col1, t], x_plane[t][:].indirect(offsets[:, col0:col1]))
+        nc.vector.tensor_copy(grouped[:, 0:C, 2], x_plane[2][:].indirect(slots(0)))
+        nc.scalar.copy(x_half2[:], x_plane[2][:])
+        nc.scalar.activation(grouped[:, C:E * C, 2], x_half2[:].indirect(slots(1)), copy)
+        for t in (0, 1):
+            nc.vector.tensor_copy(grouped[:, :, t], x_plane[t][:].indirect(offsets[:, 0:E * LIST_COLS]))
 
-        for t in range(PACK - 1):
-            gather(t, 0, E * LIST_COLS)
+        nc.scalar.copy(x_half3[:, 0:1024], x_plane[3][:, 0:1024])
+        nc.vector.tensor_copy(x_half3[:, 1024:1536], x_plane[3][:, 1024:1536])
+        nc.scalar.copy(x_half3[:, 1536:2048], x_plane[3][:, 1536:2048])
+        nc.vector.tensor_copy(grouped[:, 0:C, 3], x_plane[3][:].indirect(slots(0)))
+        nc.scalar.activation(grouped[:, C:E * C, 3], x_half3[:].indirect(slots(1)), copy)
 
-        for e in range(E):
-            gather(PACK - 1, e * LIST_COLS, (e + 1) * LIST_COLS)
-
-        for i in range(E * C // PIECE):
-            e = i * PIECE // C
-            cols = slice(i * PIECE, (i + 1) * PIECE)
+        for i, (e, first, last) in enumerate(PIECES):
+            acc = psum.tile([P, last - first], F32, name="acc%d" % i)
             nc.vector.quantize_mx(
-                out=x_code[:, cols].bitcast(FP8X4),
-                scales=x_scale[:, cols],
-                in_=grouped[:, cols, :].rearrange("p c t -> p (c t)"),
+                out=x_code[:, first:last].bitcast(FP8X4),
+                scales=x_scale[:, first:last],
+                in_=grouped[:, first:last, :].rearrange("p c t -> p (c t)"),
             )
             nc.tensor.matmul_mx(
-                out=acc[i][:],
+                out=acc[:],
                 lhsT=w_code[:, e, :].bitcast(FP8X4),
                 lhsT_scale=w_scale[:, e * N:(e + 1) * N],
-                rhs=x_code[:, cols].bitcast(FP8X4),
-                rhs_scale=x_scale[:, cols],
+                rhs=x_code[:, first:last].bitcast(FP8X4),
+                rhs_scale=x_scale[:, first:last],
                 start=True,
                 stop=True,
             )
-            nc.scalar.copy(y[e][:, i * PIECE - e * C:(i + 1) * PIECE - e * C], acc[i][:])
+            nc.scalar.copy(y[e][:, first - e * C:last - e * C], acc[:])
 
         for e in range(E):
             nc.vector.tensor_tensor(window[:].indirect(slots(e)), y[e][:], gate_sb[:, e * C:(e + 1) * C], mult)

@@ -37,13 +37,13 @@ def tile_routed_moe_kernel(tc, xT, w_words, w_scales, gate, offs, out):
         x_plane = [keep.tile([P, T], F32, name="x_plane%d" % t) for t in range(PACK)]
 
         nc.sync.dma_start(x_plane[2][:], planes[2])
+        for r in range(4):
+            nc.scalar.dma_start(
+                w_scale[r:P:32, :].rearrange("q (e n) -> q e n", e=E).bitcast(F32),
+                scale_rows[r].bitcast(F32),
+            )
         nc.sync.dma_start(offsets[:], offs)
         nc.sync.dma_start(x_plane[0][:], planes[0])
-        for r in range(4):
-            nc.sync.dma_start(
-                w_scale[r:P:32, :].rearrange("q (e n) -> q e n", e=E).bitcast(I32),
-                scale_rows[r].bitcast(I32),
-            )
         nc.sync.dma_start(x_plane[1][:], planes[1])
         for lo, hi in zip(CHUNKS, CHUNKS[1:]):
             nc.sync.dma_start(x_plane[3][:, lo:hi], planes[3][:, lo:hi])

from contextlib import ExitStack

import concourse.mybir as mybir

K, T, E, C, N = 512, 2048, 2, 256, 128
FLOPS = 2 * K * N * E * C

F32 = mybir.dt.float32
BF16 = mybir.dt.bfloat16
I32 = mybir.dt.int32
U32 = mybir.dt.uint32
U16 = mybir.dt.uint16
U8 = mybir.dt.uint8
FP8X4 = mybir.dt.float8_e4m3fn_x4

P = 128
PACK = 4
LIST_COLS = C // 16
PIECES = [(0, 0, 128), (0, 128, 256), (1, 256, 512)]
CHUNKS = [0, 1024, 1536, 2048]


def tile_routed_moe_kernel(tc, xT, w_words, w_scales, gate, offs, out):
    nc = tc.nc
    mult = mybir.AluOpType.mult
    copy = mybir.ActivationFunctionType.Copy

    with ExitStack() as ctx:
        keep = ctx.enter_context(tc.tile_pool(name="keep", bufs=1))
        psum = ctx.enter_context(tc.psum_pool(name="psum", bufs=1))

        offsets = keep.tile([P, E * LIST_COLS], U16, name="offsets")
        w_scale = keep.tile([P, E * N], U8, name="w_scale", align_bytes=64)
        scale_rows = w_scales.rearrange("e a (q r) n -> r q (e a) n", r=4)

        planes = xT.rearrange("(p t) n -> t p n", t=PACK)
        x_plane = [keep.tile([P, T], F32, name="x_plane%d" % t) for t in range(PACK)]

        nc.sync.dma_start(x_plane[2][:], planes[2])
        for r in range(4):
            nc.scalar.dma_start(
                w_scale[r:P:32, :].rearrange("q (e n) -> q e n", e=E).bitcast(F32),
                scale_rows[r].bitcast(F32),
            )
        nc.sync.dma_start(offsets[:], offs)
        nc.sync.dma_start(x_plane[0][:], planes[0])
        nc.sync.dma_start(x_plane[1][:], planes[1])
        for lo, hi in zip(CHUNKS, CHUNKS[1:]):
            nc.sync.dma_start(x_plane[3][:, lo:hi], planes[3][:, lo:hi])

        w_code = keep.tile([P, E, PACK * N], U8, name="w_code", align_bytes=64)
        nc.sync.dma_start(
            w_code[:].bitcast(I32),
            w_words.rearrange("e a p n r -> p (e a) (n r)").bitcast(I32),
        )
        gate_sb = keep.tile([P, E * C], F32, name="gate_sb")
        nc.sync.dma_start(gate_sb[:], gate)

        window = keep.tile([P, T], F32, name="window")
        nc.vector.memset(window[:], 0.0)

        x_half2 = keep.tile([P, T], BF16, name="x_half2")
        x_half3 = keep.tile([P, T], BF16, name="x_half3")
        grouped = keep.tile([P, E * C, PACK], BF16, name="grouped", align_bytes=64)
        x_code = keep.tile([P, E * C], U32, name="x_code", align_bytes=64)
        x_scale = keep.tile([P, E * C], U8, name="x_scale", align_bytes=64)
        y = [keep.tile([P, C], F32, name="y%d" % e) for e in range(E)]

        def slots(e):
            return offsets[:, e * LIST_COLS:(e + 1) * LIST_COLS]

        nc.vector.tensor_copy(grouped[:, 0:C, 2], x_plane[2][:].indirect(slots(0)))
        nc.scalar.copy(x_half2[:], x_plane[2][:])
        nc.scalar.activation(grouped[:, C:E * C, 2], x_half2[:].indirect(slots(1)), copy)
        for t in (0, 1):
            nc.vector.tensor_copy(grouped[:, :, t], x_plane[t][:].indirect(offsets[:, 0:E * LIST_COLS]))

        nc.scalar.copy(x_half3[:, 0:1024], x_plane[3][:, 0:1024])
        nc.vector.tensor_copy(x_half3[:, 1024:1536], x_plane[3][:, 1024:1536])
        nc.scalar.copy(x_half3[:, 1536:2048], x_plane[3][:, 1536:2048])
        nc.vector.tensor_copy(grouped[:, 0:C, 3], x_plane[3][:].indirect(slots(0)))
        nc.scalar.activation(grouped[:, C:E * C, 3], x_half3[:].indirect(slots(1)), copy)

        for i, (e, first, last) in enumerate(PIECES):
            acc = psum.tile([P, last - first], F32, name="acc%d" % i)
            nc.vector.quantize_mx(
                out=x_code[:, first:last].bitcast(FP8X4),
                scales=x_scale[:, first:last],
                in_=grouped[:, first:last, :].rearrange("p c t -> p (c t)"),
            )
            nc.tensor.matmul_mx(
                out=acc[:],
                lhsT=w_code[:, e, :].bitcast(FP8X4),
                lhsT_scale=w_scale[:, e * N:(e + 1) * N],
                rhs=x_code[:, first:last].bitcast(FP8X4),
                rhs_scale=x_scale[:, first:last],
                start=True,
                stop=True,
            )
            nc.scalar.copy(y[e][:, first - e * C:last - e * C], acc[:])

        for e in range(E):
            nc.vector.tensor_tensor(window[:].indirect(slots(e)), y[e][:], gate_sb[:, e * C:(e + 1) * C], mult)

        nc.sync.dma_start(out, window[:])
